import numpy as np
import ml_dtypes


def mxq(x, axis, fmt="e4m3"):
    dtype, down = {"e4m3": (ml_dtypes.float8_e4m3fn, 7), "e5m2": (ml_dtypes.float8_e5m2, 14)}[fmt]
    v = np.moveaxis(np.asarray(x, np.float32).astype(ml_dtypes.bfloat16).astype(np.float64), axis, -1)
    blocks = v.reshape(v.shape[:-1] + (-1, 32))
    amax = np.abs(blocks).max(-1, keepdims=True)
    byte = np.maximum(np.where(amax > 0, np.frexp(amax)[1] - 1 + 127, 0) - down, 1)
    scale = np.exp2(byte - 127.0)
    codes = (blocks / scale).astype(np.float32).astype(dtype).astype(np.float64)
    return np.moveaxis((codes * scale).reshape(v.shape), -1, axis)


WIDE = False


def mx_kscale(k):
    if not WIDE:
        return np.ones(k)
    levels = np.array([10, -10, 5, -5, 0])
    if k % 512:
        return np.exp2(np.random.permutation(np.resize(levels, k // 32))).repeat(32)
    a = np.empty((k // 512, 16))
    for p in range(k // 512):
        a[p, :8] = np.random.permutation(np.resize(levels, 8))
        for g in range(8):
            far = levels[np.abs(levels - a[p, g]) >= 10]
            a[p, g + 8] = far[np.random.randint(len(far))]
    return np.exp2(a.ravel()).repeat(32)


BF16 = ml_dtypes.bfloat16


def bf(x):
    return np.asarray(x, np.float32).astype(BF16)


def f64(x):
    return np.asarray(x).astype(np.float64)


E2M1 = np.array([0.0, 0.5, 1.0, 1.5, 2.0, 3.0, 4.0, 6.0, -0.0, -0.5, -1.0, -1.5, -2.0, -3.0, -4.0, -6.0])


def pack_weight(w, fmt):
    k, n = w.shape
    w = f64(bf(w)).reshape(k // 32, 32, n)
    amax = np.abs(w).max(1)
    if fmt == "e4m3":
        byte = np.frexp(amax)[1] - 1 + 127 - 7
    else:
        mant, ex = np.frexp(amax / 6.0)
        byte = np.where(mant > 0.5, ex, ex - 1) + 127
    byte = np.clip(np.where(amax > 0, byte, 1), 1, 254)
    scaled = (w * np.exp2(127.0 - byte)[:, None, :]).reshape(k, n).astype(np.float32)
    by_word = np.ascontiguousarray(scaled.reshape(k // 512, 128, 4, n).transpose(0, 1, 3, 2))
    if fmt == "e4m3":
        words = by_word.astype(ml_dtypes.float8_e4m3fn).view(np.uint8)
    else:
        c = by_word.astype(ml_dtypes.float4_e2m1fn).view(np.uint8) & 0xF
        words = c[..., 0::2] | (c[..., 1::2] << 4)
    return np.ascontiguousarray(words), np.ascontiguousarray(byte.astype(np.uint8).reshape(k // 512, 16, n))


def unpack_weight(words, scales, fmt):
    g, p, n, _ = words.shape
    if fmt == "e4m3":
        vals = np.ascontiguousarray(words).view(ml_dtypes.float8_e4m3fn).astype(np.float64)
    else:
        nib = np.empty((g, p, n, 4), np.uint8)
        nib[..., 0::2] = words & 0xF
        nib[..., 1::2] = words >> 4
        vals = E2M1[nib]
    vals = vals * np.repeat(np.exp2(scales.astype(np.float64) - 127.0), 8, axis=1)[..., None]
    return vals.transpose(0, 1, 3, 2).reshape(g * 512, n)
def pack4(w):
    words, scales = pack_weight(w, "e2m1")
    return words.reshape(words.shape[0], 128, -1), scales


def unpack4(words, scales):
    return unpack_weight(words.reshape(words.shape[0], 128, -1, 2), scales, "e2m1")


M, H, F = 1024, 1536, 512


def setup_inputs():
    s, u = mx_kscale(H), mx_kscale(M)
    bt = np.random.standard_normal((H, H)) / (3 * np.sqrt(H)) / s[:, None] * s
    c = np.random.standard_normal((M, M)) / (3 * np.sqrt(M)) / u[:, None] * u
    at = np.random.standard_normal((H, F)) / np.sqrt(H) / s[:, None]
    bt_words, bt_scales = pack4(bt)
    c_words, c_scales = pack4(c)
    at_words, at_scales = pack4(at)
    return {"dy": bf(np.random.standard_normal((M, H)) * s * u[:, None]),
            "z": bf(np.random.standard_normal((M, H))),
            "leak": bf(0.25 + 0.05 * np.random.standard_normal(H)),
            "r": bf((1 + 0.1 * np.random.standard_normal(M)) / u),
            "bt_words": bt_words, "bt_scales": bt_scales,
            "c_words": c_words, "c_scales": c_scales,
            "at_words": at_words, "at_scales": at_scales}


def reference(dy, z, leak, r, bt_words, bt_scales, c_words, c_scales, at_words, at_scales):
    dy = f64(dy)
    d1 = dy + (mxq(dy, 1, "e4m3") @ unpack4(bt_words, bt_scales))
    d2 = d1 + (unpack4(c_words, c_scales).T @ mxq(d1, 0, "e4m3"))
    slope = np.where(f64(z) > 0, 1.0, f64(leak))
    dz = d2 * f64(r)[:, None] * slope
    return mxq(dz, 1, "e4m3") @ unpack4(at_words, at_scales)

@@ -1,0 +1,431 @@
+from contextlib import ExitStack
+
+import concourse.mybir as mybir
+from concourse.masks import make_identity
+
+F32 = mybir.dt.float32
+BF16 = mybir.dt.bfloat16
+I32 = mybir.dt.int32
+U32 = mybir.dt.uint32
+U8 = mybir.dt.uint8
+FP8X4 = mybir.dt.float8_e4m3fn_x4
+FP4X4 = mybir.dt.float4_e2m1fn_x4
+ADD = mybir.AluOpType.add
+MULT = mybir.AluOpType.mult
+IS_GT = mybir.AluOpType.is_gt
+IDENTITY = mybir.ActivationFunctionType.Identity
+COPY = mybir.ActivationFunctionType.Copy
+
+M, H, F = 1024, 1536, 512
+P = 128
+PACK = 4
+KP = P * PACK
+MG = M // KP
+HG = H // KP
+
+FLOPS = 2 * M * H * H + 2 * M * M * H + 2 * M * H * F
+
+
+def tile_residual_prelu_layer_backward_t2_kernel(
+    tc, dy, z, leak, r, bt_words, bt_scales, c_words, c_scales, at_words, at_scales, out
+):
+    nc = tc.nc
+    with ExitStack() as ctx:
+        keep = ctx.enter_context(tc.tile_pool(name="keep", bufs=1))
+        stage = ctx.enter_context(tc.tile_pool(name="stage", bufs=3))
+        ps_mm = ctx.enter_context(tc.psum_pool(name="ps_mm", bufs=4))
+        ps_tr = ctx.enter_context(tc.psum_pool(name="ps_tr", bufs=3))
+        ps_out = ctx.enter_context(tc.psum_pool(name="ps_out", bufs=1))
+        ctx.enter_context(tc.manual_schedule())
+
+        dy_sb = [keep.tile([P, PACK, H], BF16, name=f"dy_sb{g}", tag="rows", bufs=MG, align_bytes=64) for g in range(MG)]
+        z_sb = [keep.tile([P, PACK, H], BF16, name=f"z_sb{g}", tag="zrows", bufs=MG, align_bytes=64) for g in range(MG)]
+        bt = keep.tile([P, HG, 2 * H], U8, name="bt", align_bytes=64)
+        bt_s = keep.tile([P, HG, H], U8, name="bt_s", align_bytes=64)
+        c_in = keep.tile([P, MG, 2 * M], U8, name="c_in", align_bytes=64)
+        c_in_s = keep.tile([P, MG, M], U8, name="c_in_s", align_bytes=64)
+        cp = keep.tile([P, MG, 2 * M], U8, name="cp", align_bytes=64)
+        cp_s = keep.tile([P, MG, M], U8, name="cp_s", align_bytes=64)
+        at = keep.tile([P, HG, 2 * F], U8, name="at", align_bytes=64)
+        at_s = keep.tile([P, HG, F], U8, name="at_s", align_bytes=64)
+        ident = keep.tile([P, P], F32, name="ident", align_bytes=64)
+        leak_in = keep.tile([P, HG, PACK], BF16, name="leak_in")
+        r_in = keep.tile([P, MG, PACK], BF16, name="r_in")
+        leak_col = keep.tile([P, HG, PACK], F32, name="leak_col")
+        oml_col = keep.tile([P, HG, PACK], F32, name="oml_col")
+        r_col = keep.tile([P, MG, PACK], F32, name="r_col")
+        warm = keep.tile([P, 1], F32, name="warm")
+        dyq = keep.tile([P, MG, HG, KP], U32, name="dyq", align_bytes=64)
+        dyq_s = keep.tile([P, MG, HG, KP], U8, name="dyq_s", align_bytes=64)
+        d1 = [keep.tile([P, PACK, H], F32, name=f"d1_{g}", align_bytes=64) for g in range(MG)]
+        d1q = keep.tile([P, MG, H], U32, name="d1q", align_bytes=64)
+        d1q_s = keep.tile([P, MG, H], U8, name="d1q_s", align_bytes=64)
+        slope = [keep.tile([P, PACK, M], BF16, name=f"slope{f}", align_bytes=64) for f in range(HG)]
+
+        nc.vector.memset(bt_s[:].rearrange("p g n -> p (g n)").bitcast(I32), 0)
+        nc.gpsimd.memset(warm[:], 0.0)
+        make_identity(nc, ident[:])
+        nc.scalar.activation(out=warm[:], in_=warm[:], func=IDENTITY)
+
+        dy_v = dy.rearrange("(g p t) h -> g p t h", g=MG, t=PACK)
+        z_v = z.rearrange("(g p t) h -> g p t h", g=MG, t=PACK)
+        out_v = out.rearrange("(g p t) n -> g p t n", g=MG, t=PACK)
+
+        def load_dy(g, f, t0, t1):
+            cols = slice(KP * f, KP * (f + 1))
+            nc.sync.dma_start(out=dy_sb[g][:, t0:t1, cols], in_=dy_v[g][:, t0:t1, cols])
+
+        def load_words(tile, words, g):
+            nc.sync.dma_start(out=tile[:, g, :].bitcast(I32), in_=words[g].bitcast(I32))
+
+        def load_scales(queue, tile, scales):
+            src = scales.bitcast(I32)
+            for q in range(4):
+                queue.dma_start(
+                    out=tile[32 * q : 32 * q + 4, :, :].bitcast(I32),
+                    in_=src[:, 4 * q : 4 * q + 4, :].rearrange("g q n -> q g n"),
+                )
+
+        load_dy(0, 0, 0, 2)
+        load_dy(0, 0, 2, 4)
+        load_scales(nc.gpsimd, bt_s, bt_scales)
+        load_dy(0, 1, 0, 4)
+        load_words(bt, bt_words, 0)
+        load_dy(0, 2, 0, 4)
+        load_words(bt, bt_words, 1)
+        load_words(bt, bt_words, 2)
+        nc.gpsimd.dma_start(out=leak_in[:], in_=leak.rearrange("(f p t) -> p f t", f=HG, t=PACK))
+        nc.gpsimd.dma_start(out=r_in[:], in_=r.rearrange("(g p t) -> p g t", g=MG, t=PACK))
+        nc.gpsimd.memset(c_in_s[:].rearrange("p g n -> p (g n)").bitcast(I32), 0)
+        nc.gpsimd.memset(at_s[:].rearrange("p g n -> p (g n)").bitcast(I32), 0)
+        load_dy(1, 0, 0, 4)
+        load_scales(nc.sync, c_in_s, c_scales)
+        for g in range(MG):
+            load_words(c_in, c_words, g)
+        load_dy(1, 1, 0, 4)
+        load_dy(1, 2, 0, 4)
+        nc.sync.dma_start(out=z_sb[0][:], in_=z_v[0])
+        nc.sync.dma_start(out=z_sb[1][:], in_=z_v[1])
+        load_scales(nc.sync, at_s, at_scales)
+        for f in range(HG):
+            load_words(at, at_words, f)
+
+        def dy_transposes(g, f):
+            words = dy_sb[g][:].rearrange("p t h -> p (t h)").bitcast(F32).rearrange("p (t w) -> p t w", t=PACK)
+            banks = []
+            for half in range(2):
+                tr = ps_tr.tile([P, 2, 2 * P], F32, name="tr")
+                for j in range(2):
+                    for u in range(2):
+                        lo = KP // 2 * f + u
+                        nc.tensor.transpose(
+                            tr[:, u, P * j : P * (j + 1)], words[:, 2 * half + j, lo : KP // 2 * (f + 1) : 2], ident[:]
+                        )
+                banks.append(tr)
+            return banks
+
+        def dy_copy_quant(g, f, banks, engines):
+            tiles = []
+            for half in range(2):
+                dyt = stage.tile([P, 2 * P, PACK], BF16, name="dyt", bufs=6, align_bytes=64)
+                dst = dyt[:].rearrange("p m j -> p (m j)").bitcast(F32).rearrange("p (m u) -> p m u", u=2)
+                src = banks[half][:].rearrange("p u m -> p m u")
+                if engines[half] == "s":
+                    nc.scalar.copy(out=dst, in_=src)
+                else:
+                    nc.vector.tensor_copy(out=dst, in_=src)
+                tiles.append(dyt)
+            return tiles
+
+        def dy_quant(g, f, tiles):
+            for half in range(2):
+                cols = slice(2 * P * half, 2 * P * (half + 1))
+                nc.vector.quantize_mx(
+                    out=dyq[:, g, f, cols].bitcast(FP8X4),
+                    scales=dyq_s[:, g, f, cols],
+                    in_=tiles[half][:].rearrange("p m j -> p (m j)"),
+                )
+
+        def mx1(acc, g, n, t, f):
+            rows = slice(P * t, P * (t + 1))
+            nc.tensor.matmul_mx(
+                out=acc[:],
+                lhsT=dyq[:, g, f, rows].bitcast(FP8X4),
+                lhsT_scale=dyq_s[:, g, f, rows],
+                rhs=bt[:, f, 2 * KP * n : 2 * KP * (n + 1)].bitcast(FP4X4),
+                rhs_scale=bt_s[:, f, KP * n : KP * (n + 1)],
+                start=(f == 0),
+                stop=(f == HG - 1),
+            )
+
+        def add_dy(acc, g, n, t):
+            cols = slice(KP * n, KP * (n + 1))
+            nc.vector.tensor_tensor(
+                out=d1[g][:, t, cols].rearrange("p (k q) -> p k q", k=PACK),
+                in0=acc[:].rearrange("p (q k) -> p k q", k=PACK),
+                in1=dy_sb[g][:, t, cols].rearrange("p (q k) -> p k q", k=PACK),
+                op=ADD,
+            )
+
+        def unit1(g, n, t):
+            acc = ps_mm.tile([P, KP], F32, name="acc")
+            for f in range(HG):
+                mx1(acc, g, n, t, f)
+            add_dy(acc, g, n, t)
+
+        grouped = {}
+
+        def interleave_d1(g, n, parts):
+            d1t = stage.tile([P, KP, PACK], BF16, name="d1t", bufs=3, align_bytes=64)
+            grouped[g, n] = d1t
+            for eng, c0, c1 in parts:
+                src = d1[g][:, :, KP * n + c0 : KP * n + c1].rearrange("p t c -> p c t")
+                if eng == "s":
+                    nc.scalar.copy(out=d1t[:, c0:c1, :], in_=src)
+                else:
+                    nc.vector.tensor_copy(out=d1t[:, c0:c1, :], in_=src)
+
+        def quant_d1(g, n):
+            cols = slice(KP * n, KP * (n + 1))
+            nc.vector.quantize_mx(
+                out=d1q[:, g, cols].bitcast(FP8X4),
+                scales=d1q_s[:, g, cols],
+                in_=grouped[g, n][:].rearrange("p c t -> p (c t)"),
+            )
+
+        def scale_d1(g, t, eng):
+            if eng == "s":
+                nc.scalar.activation(out=d1[g][:, t, :], in_=d1[g][:, t, :], func=COPY, scale=r_col[:, g, t : t + 1])
+            else:
+                for n in range(HG):
+                    cols = slice(KP * n, KP * (n + 1))
+                    nc.gpsimd.tensor_scalar(
+                        out=d1[g][:, t, cols], in0=d1[g][:, t, cols],
+                        scalar1=r_col[:, g, t : t + 1], scalar2=0.0, op0=MULT, op1=ADD,
+                    )
+
+        mask = {}
+
+        def make_mask(g, t):
+            if t == 0:
+                mask[g] = keep.tile([P, PACK, 2, H // 2], BF16, name=f"mask{g}", tag="rows" if g == 0 else "zrows", bufs=MG, align_bytes=64)
+            (nc.vector if g == 0 else nc.gpsimd).tensor_scalar(
+                out=mask[g][:, t, :, :].rearrange("p u (q e) -> p u q e", e=2),
+                in0=z_sb[g][:, t, :].rearrange("p (q u e) -> p u q e", u=2, e=2),
+                scalar1=0.0, scalar2=1.0, op0=IS_GT, op1=MULT,
+            )
+
+        def mask_transposes(g, f, u):
+            words = mask[g][:].rearrange("p t u c -> p (t u c)").bitcast(F32).rearrange("p (t u w) -> p t u w", t=PACK, u=2)
+            tr = ps_tr.tile([P, PACK, P], F32, name="tr")
+            for t in range(PACK):
+                nc.tensor.transpose(tr[:, t, :], words[:, t, u, P * f : P * (f + 1)], ident[:])
+            return tr
+
+        def make_slope(g, f, u, tr):
+            pairs = tr[:].rearrange("p t m -> p (t m)").bitcast(BF16)
+            for e in range(2):
+                k = 2 * u + e
+                nc.scalar.activation(
+                    out=slope[f][:, k, KP * g : KP * (g + 1)],
+                    in_=pairs[:, e : 2 * KP : 2],
+                    func=IDENTITY,
+                    bias=leak_col[:, f, k : k + 1],
+                    scale=oml_col[:, f, k : k + 1],
+                )
+
+        def mask_unit(g, f, u):
+            make_slope(g, f, u, mask_transposes(g, f, u))
+
+        def permute_c(gk, gm):
+            a, b = 2 * KP * gm, 2 * KP * (gm + 1)
+            nc.gpsimd.tensor_copy(
+                out=cp[:, gk, a:b].rearrange("p (t m b) -> p t m b", t=PACK, b=2),
+                in_=c_in[:, gk, a:b].rearrange("p (m t b) -> p t m b", t=PACK, b=2),
+            )
+
+        def permute_c_scales(gk, gm):
+            a, b = KP * gm, KP * (gm + 1)
+            nc.gpsimd.tensor_copy(
+                out=cp_s[:, gk, a:b].rearrange("p (t m) -> p t m", t=PACK),
+                in_=c_in_s[:, gk, a:b].rearrange("p (m t) -> p t m", t=PACK),
+            )
+
+        accs, vs, vts, dzs, dzqs = {}, {}, {}, {}, {}
+
+        def mx2(j, f):
+            g, t = divmod(j, PACK)
+            acc = ps_mm.tile([P, KP], F32, name="acc")
+            lo = KP * g + P * t
+            for gk in range(MG):
+                nc.tensor.matmul_mx(
+                    out=acc[:],
+                    lhsT=cp[:, gk, 2 * lo : 2 * (lo + P)].bitcast(FP4X4),
+                    lhsT_scale=cp_s[:, gk, lo : lo + P],
+                    rhs=d1q[:, gk, KP * f : KP * (f + 1)].bitcast(FP8X4),
+                    rhs_scale=d1q_s[:, gk, KP * f : KP * (f + 1)],
+                    start=(gk == 0),
+                    stop=(gk == MG - 1),
+                )
+            accs[j, f] = acc
+
+        def finish_d2(j, f):
+            g, t = divmod(j, PACK)
+            v = stage.tile([P, KP], F32, name="v", bufs=8, align_bytes=64)
+            nc.vector.scalar_tensor_tensor(
+                out=v[:], in0=accs[j, f][:], scalar=r_col[:, g, t : t + 1],
+                in1=d1[g][:, t, KP * f : KP * (f + 1)], op0=MULT, op1=ADD,
+            )
+            vs[j, f] = v
+
+        def v_transposes(j, f):
+            vt = ps_tr.tile([P, PACK, P], F32, name="tr")
+            for k in range(PACK):
+                nc.tensor.transpose(vt[:, k, :], vs[j, f][:, P * k : P * (k + 1)], ident[:])
+            vts[j, f] = vt
+
+        def make_dz(j, f):
+            dz = stage.tile([P, P, PACK], BF16, name="dz", bufs=6, align_bytes=64)
+            nc.vector.tensor_tensor(
+                out=dz[:],
+                in0=vts[j, f][:].rearrange("p k m -> p m k"),
+                in1=slope[f][:, :, P * j : P * (j + 1)].rearrange("p k m -> p m k"),
+                op=MULT,
+            )
+            dzs[j, f] = dz
+
+        def quant_dz(j, f):
+            codes = stage.tile([P, P], U32, name="dzq", bufs=9, align_bytes=64)
+            scales = stage.tile([P, P], U8, name="dzq_s", bufs=9, align_bytes=64)
+            nc.vector.quantize_mx(
+                out=codes[:].bitcast(FP8X4), scales=scales[:], in_=dzs[j, f][:].rearrange("p m k -> p (m k)")
+            )
+            dzqs[j, f] = (codes, scales)
+
+        def mx3(j):
+            po = ps_out.tile([P, F], F32, name="po")
+            for f in range(HG):
+                codes, scales = dzqs[j, f]
+                nc.tensor.matmul_mx(
+                    out=po[:],
+                    lhsT=codes[:].bitcast(FP8X4),
+                    lhsT_scale=scales[:],
+                    rhs=at[:, f, :].bitcast(FP4X4),
+                    rhs_scale=at_s[:, f, :],
+                    start=(f == 0),
+                    stop=(f == HG - 1),
+                )
+            return po
+
+        def store(j, po):
+            g, t = divmod(j, PACK)
+            res = stage.tile([P, F], F32, name="res", bufs=3, align_bytes=64)
+            nc.scalar.copy(out=res[:], in_=po[:])
+            nc.sync.dma_start(out=out_v[g][:, t, :], in_=res[:])
+
+        b00 = dy_copy_quant(0, 0, dy_transposes(0, 0), "sv")
+        dy_quant(0, 0, b00)
+        b01 = dy_copy_quant(0, 1, dy_transposes(0, 1), "sv")
+        dy_quant(0, 1, b01)
+        nc.gpsimd.tensor_copy(out=leak_col[:], in_=leak_in[:])
+        nc.gpsimd.tensor_scalar(out=oml_col[:], in0=leak_in[:], scalar1=-1.0, scalar2=1.0, op0=MULT, op1=ADD)
+        nc.gpsimd.tensor_copy(out=r_col[:], in_=r_in[:])
+        first = [ps_mm.tile([P, KP], F32, name="acc") for t in range(PACK)]
+        for t in range(PACK):
+            mx1(first[t], 0, 0, t, 0)
+        b02 = dy_copy_quant(0, 2, dy_transposes(0, 2), "ss")
+        dy_quant(0, 2, b02)
+        for t in range(PACK):
+            mx1(first[t], 0, 0, t, 1)
+        for t in range(PACK):
+            mx1(first[t], 0, 0, t, 2)
+            add_dy(first[t], 0, 0, t)
+        interleave_d1(0, 0, [("s", 0, KP)])
+        unit1(0, 1, 0)
+        unit1(0, 1, 1)
+        b10 = dy_copy_quant(1, 0, dy_transposes(1, 0), "ss")
+        unit1(0, 1, 2)
+        quant_d1(0, 0)
+        unit1(0, 1, 3)
+        dy_quant(1, 0, b10)
+        interleave_d1(0, 1, [("s", 0, KP)])
+        unit1(0, 2, 0)
+        b11 = dy_copy_quant(1, 1, dy_transposes(1, 1), "ss")
+        for gk in range(MG):
+            permute_c(gk, 0)
+            permute_c_scales(gk, 0)
+        unit1(0, 2, 1)
+        quant_d1(0, 1)
+        unit1(0, 2, 2)
+        dy_quant(1, 1, b11)
+        b12 = dy_copy_quant(1, 2, dy_transposes(1, 2), "ss")
+        unit1(0, 2, 3)
+        interleave_d1(0, 2, [("s", 0, KP)])
+        dy_quant(1, 2, b12)
+        for t in range(PACK):
+            make_mask(0, t)
+            unit1(1, 0, t)
+        quant_d1(0, 2)
+        interleave_d1(1, 0, [("s", 0, KP)])
+        mask_unit(0, 0, 0)
+        mask_unit(0, 0, 1)
+        unit1(1, 1, 0)
+        unit1(1, 1, 1)
+        scale_d1(0, 0, "g")
+        quant_d1(1, 0)
+        unit1(1, 1, 2)
+        mask_unit(0, 1, 0)
+        mask_unit(0, 1, 1)
+        unit1(1, 1, 3)
+        for t in range(PACK):
+            make_mask(1, t)
+        scale_d1(0, 1, "g")
+        interleave_d1(1, 1, [("s", 0, KP)])
+        unit1(1, 2, 0)
+        mask_unit(0, 2, 0)
+        unit1(1, 2, 1)
+        unit1(1, 2, 2)
+        quant_d1(1, 1)
+        unit1(1, 2, 3)
+        mx2(0, 0)
+        mx2(0, 1)
+        interleave_d1(1, 2, [("s", 0, 208), ("v", 208, KP)])
+        mask_unit(0, 2, 1)
+        finish_d2(0, 0)
+        mx2(1, 0)
+        quant_d1(1, 2)
+        for gk in range(MG):
+            permute_c(gk, 1)
+            permute_c_scales(gk, 1)
+
+        units = [(0, 0), (0, 1), (1, 0), (1, 1), (0, 2), (1, 2)]
+        units += [(j, f) for j in range(2, M // P) for f in range(HG)]
+        groups = [units[i : i + 3] for i in range(0, len(units), 3)]
+        pe_extra = {1: [(1, 0, 0)], 2: [(1, 0, 1), (1, 1, 0)], 3: [(1, 1, 1)], 4: [(1, 2, 0), (1, 2, 1)]}
+        ready = {3: 1, 4: 2, 5: 3, 6: 4, 7: 5, 8: 6, 9: 7}
+        s_scale = {0: [2], 1: [3], 2: [4], 3: [5], 4: [6], 5: [7]}
+        for i in range(len(groups) + 2):
+            now = groups[i] if i < len(groups) else []
+            prev = groups[i - 1] if 1 <= i <= len(groups) else []
+            if i > 0:
+                for j, f in now:
+                    mx2(j, f)
+            for j, f in prev:
+                v_transposes(j, f)
+            if i == 3:
+                store(0, mx3(0))
+            for args in pe_extra.get(i, []):
+                mask_unit(*args)
+            for x in range(3):
+                if now and (i > 0 or x > 0):
+                    finish_d2(*now[x])
+                if prev:
+                    make_dz(*prev[x])
+                    if x > 0:
+                        quant_dz(*prev[x - 1])
+            if prev:
+                quant_dz(*prev[2])
+            if i in ready:
+                store(ready[i], mx3(ready[i]))
+            for j in s_scale.get(i, []):
+                scale_d1(j // PACK, j % PACK, "s")

@@ -64,6 +64,8 @@ def tile_residual_prelu_layer_backward_t2_kernel(
 
         nc.vector.memset(bt_s[:].rearrange("p g n -> p (g n)").bitcast(I32), 0)
         nc.gpsimd.memset(warm[:], 0.0)
+        nc.vector.memset(c_in_s[:].rearrange("p g n -> p (g n)").bitcast(I32), 0)
+        nc.vector.memset(at_s[:].rearrange("p g n -> p (g n)").bitcast(I32), 0)
         make_identity(nc, ident[:])
         nc.scalar.activation(out=warm[:], in_=warm[:], func=IDENTITY)
 
@@ -94,14 +96,12 @@ def tile_residual_prelu_layer_backward_t2_kernel(
         load_dy(0, 2, 0, 4)
         load_words(bt, bt_words, 1)
         load_words(bt, bt_words, 2)
-        nc.gpsimd.dma_start(out=leak_in[:], in_=leak.rearrange("(f p t) -> p f t", f=HG, t=PACK))
-        nc.gpsimd.dma_start(out=r_in[:], in_=r.rearrange("(g p t) -> p g t", g=MG, t=PACK))
-        nc.gpsimd.memset(c_in_s[:].rearrange("p g n -> p (g n)").bitcast(I32), 0)
-        nc.gpsimd.memset(at_s[:].rearrange("p g n -> p (g n)").bitcast(I32), 0)
-        load_dy(1, 0, 0, 4)
         load_scales(nc.sync, c_in_s, c_scales)
         for g in range(MG):
             load_words(c_in, c_words, g)
+        nc.gpsimd.dma_start(out=leak_in[:], in_=leak.rearrange("(f p t) -> p f t", f=HG, t=PACK))
+        nc.gpsimd.dma_start(out=r_in[:], in_=r.rearrange("(g p t) -> p g t", g=MG, t=PACK))
+        load_dy(1, 0, 0, 4)
         load_dy(1, 1, 0, 4)
         load_dy(1, 2, 0, 4)
         nc.sync.dma_start(out=z_sb[0][:], in_=z_v[0])
@@ -209,10 +209,10 @@ def tile_residual_prelu_layer_backward_t2_kernel(
         def make_mask(g, t):
             if t == 0:
                 mask[g] = keep.tile([P, PACK, 2, H // 2], BF16, name=f"mask{g}", tag="rows" if g == 0 else "zrows", bufs=MG, align_bytes=64)
-            (nc.vector if g == 0 else nc.gpsimd).tensor_scalar(
+            nc.vector.tensor_scalar(
                 out=mask[g][:, t, :, :].rearrange("p u (q e) -> p u q e", e=2),
                 in0=z_sb[g][:, t, :].rearrange("p (q u e) -> p u q e", u=2, e=2),
-                scalar1=0.0, scalar2=1.0, op0=IS_GT, op1=MULT,
+                scalar1=0.0, scalar2=None, op0=IS_GT,
             )
 
         def mask_transposes(g, f, u):
@@ -239,14 +239,14 @@ def tile_residual_prelu_layer_backward_t2_kernel(
 
         def permute_c(gk, gm):
             a, b = 2 * KP * gm, 2 * KP * (gm + 1)
-            nc.gpsimd.tensor_copy(
+            nc.vector.tensor_copy(
                 out=cp[:, gk, a:b].rearrange("p (t m b) -> p t m b", t=PACK, b=2),
                 in_=c_in[:, gk, a:b].rearrange("p (m t b) -> p t m b", t=PACK, b=2),
             )
 
         def permute_c_scales(gk, gm):
             a, b = KP * gm, KP * (gm + 1)
-            nc.gpsimd.tensor_copy(
+            nc.vector.tensor_copy(
                 out=cp_s[:, gk, a:b].rearrange("p (t m) -> p t m", t=PACK),
                 in_=c_in_s[:, gk, a:b].rearrange("p (m t) -> p t m", t=PACK),
             )
@@ -325,7 +325,7 @@ def tile_residual_prelu_layer_backward_t2_kernel(
 
         b00 = dy_copy_quant(0, 0, dy_transposes(0, 0), "sv")
         dy_quant(0, 0, b00)
-        b01 = dy_copy_quant(0, 1, dy_transposes(0, 1), "sv")
+        b01 = dy_copy_quant(0, 1, dy_transposes(0, 1), "ss")
         dy_quant(0, 1, b01)
         nc.gpsimd.tensor_copy(out=leak_col[:], in_=leak_in[:])
         nc.gpsimd.tensor_scalar(out=oml_col[:], in0=leak_in[:], scalar1=-1.0, scalar2=1.0, op0=MULT, op1=ADD)
@@ -342,61 +342,70 @@ def tile_residual_prelu_layer_backward_t2_kernel(
             add_dy(first[t], 0, 0, t)
         interleave_d1(0, 0, [("s", 0, KP)])
         unit1(0, 1, 0)
+        permute_c(0, 0)
         unit1(0, 1, 1)
+        permute_c(1, 0)
+        permute_c_scales(0, 0)
         b10 = dy_copy_quant(1, 0, dy_transposes(1, 0), "ss")
         unit1(0, 1, 2)
         quant_d1(0, 0)
         unit1(0, 1, 3)
+        permute_c_scales(1, 0)
+        permute_c(0, 1)
         dy_quant(1, 0, b10)
         interleave_d1(0, 1, [("s", 0, KP)])
         unit1(0, 2, 0)
         b11 = dy_copy_quant(1, 1, dy_transposes(1, 1), "ss")
-        for gk in range(MG):
-            permute_c(gk, 0)
-            permute_c_scales(gk, 0)
         unit1(0, 2, 1)
+        permute_c(1, 1)
         quant_d1(0, 1)
         unit1(0, 2, 2)
         dy_quant(1, 1, b11)
+        for gk in range(MG):
+            permute_c_scales(gk, 1)
         b12 = dy_copy_quant(1, 2, dy_transposes(1, 2), "ss")
         unit1(0, 2, 3)
         interleave_d1(0, 2, [("s", 0, KP)])
         dy_quant(1, 2, b12)
-        for t in range(PACK):
-            make_mask(0, t)
-            unit1(1, 0, t)
+        make_mask(0, 0)
+        make_mask(0, 1)
+        unit1(1, 0, 0)
+        unit1(1, 0, 1)
+        make_mask(0, 2)
+        make_mask(0, 3)
+        unit1(1, 0, 2)
+        unit1(1, 0, 3)
         quant_d1(0, 2)
-        interleave_d1(1, 0, [("s", 0, KP)])
         mask_unit(0, 0, 0)
         mask_unit(0, 0, 1)
+        interleave_d1(1, 0, [("s", 0, KP)])
         unit1(1, 1, 0)
         unit1(1, 1, 1)
-        scale_d1(0, 0, "g")
-        quant_d1(1, 0)
+        make_mask(1, 0)
+        make_mask(1, 1)
         unit1(1, 1, 2)
+        quant_d1(1, 0)
         mask_unit(0, 1, 0)
         mask_unit(0, 1, 1)
         unit1(1, 1, 3)
-        for t in range(PACK):
-            make_mask(1, t)
-        scale_d1(0, 1, "g")
         interleave_d1(1, 1, [("s", 0, KP)])
+        make_mask(1, 2)
+        make_mask(1, 3)
         unit1(1, 2, 0)
         mask_unit(0, 2, 0)
         unit1(1, 2, 1)
         unit1(1, 2, 2)
         quant_d1(1, 1)
         unit1(1, 2, 3)
+        scale_d1(0, 0, "s")
         mx2(0, 0)
         mx2(0, 1)
         interleave_d1(1, 2, [("s", 0, 208), ("v", 208, KP)])
+        scale_d1(0, 1, "s")
         mask_unit(0, 2, 1)
         finish_d2(0, 0)
         mx2(1, 0)
         quant_d1(1, 2)
-        for gk in range(MG):
-            permute_c(gk, 1)
-            permute_c_scales(gk, 1)
 
         units = [(0, 0), (0, 1), (1, 0), (1, 1), (0, 2), (1, 2)]
         units += [(j, f) for j in range(2, M // P) for f in range(HG)]

@@ -10,11 +10,8 @@ U32 = mybir.dt.uint32
 U8 = mybir.dt.uint8
 FP8X4 = mybir.dt.float8_e4m3fn_x4
 FP4X4 = mybir.dt.float4_e2m1fn_x4
-ADD = mybir.AluOpType.add
-MULT = mybir.AluOpType.mult
-IS_GT = mybir.AluOpType.is_gt
-IDENTITY = mybir.ActivationFunctionType.Identity
-COPY = mybir.ActivationFunctionType.Copy
+ALU = mybir.AluOpType
+ACT = mybir.ActivationFunctionType
 
 M, H, F = 1024, 1536, 512
 P = 128
@@ -22,6 +19,7 @@ PACK = 4
 KP = P * PACK
 MG = M // KP
 HG = H // KP
+PAIR = 2
 
 FLOPS = 2 * M * H * H + 2 * M * M * H + 2 * M * H * F
 
@@ -32,42 +30,42 @@ def tile_residual_prelu_layer_backward_t2_kernel(
     nc = tc.nc
     with ExitStack() as ctx:
         keep = ctx.enter_context(tc.tile_pool(name="keep", bufs=1))
-        stage = ctx.enter_context(tc.tile_pool(name="stage", bufs=3))
-        ps_mm = ctx.enter_context(tc.psum_pool(name="ps_mm", bufs=4))
+        stage = ctx.enter_context(tc.tile_pool(name="stage", bufs=2))
+        ps_acc = ctx.enter_context(tc.psum_pool(name="ps_acc", bufs=5))
         ps_tr = ctx.enter_context(tc.psum_pool(name="ps_tr", bufs=3))
-        ps_out = ctx.enter_context(tc.psum_pool(name="ps_out", bufs=1))
         ctx.enter_context(tc.manual_schedule())
-
-        dy_sb = [keep.tile([P, PACK, H], BF16, name=f"dy_sb{g}", tag="rows", bufs=MG, align_bytes=64) for g in range(MG)]
-        z_sb = [keep.tile([P, PACK, H], BF16, name=f"z_sb{g}", tag="zrows", bufs=MG, align_bytes=64) for g in range(MG)]
+        dy_sb = keep.tile([P, MG, PACK, H], BF16, name="dy_sb", align_bytes=64)
+        z_sb = keep.tile([P, MG, PACK, H], BF16, name="z_sb", align_bytes=64)
         bt = keep.tile([P, HG, 2 * H], U8, name="bt", align_bytes=64)
         bt_s = keep.tile([P, HG, H], U8, name="bt_s", align_bytes=64)
         c_in = keep.tile([P, MG, 2 * M], U8, name="c_in", align_bytes=64)
         c_in_s = keep.tile([P, MG, M], U8, name="c_in_s", align_bytes=64)
-        cp = keep.tile([P, MG, 2 * M], U8, name="cp", align_bytes=64)
-        cp_s = keep.tile([P, MG, M], U8, name="cp_s", align_bytes=64)
+        c = keep.tile([P, MG, 2 * M], U8, name="c", align_bytes=64)
+        c_s = keep.tile([P, MG, M], U8, name="c_s", align_bytes=64)
         at = keep.tile([P, HG, 2 * F], U8, name="at", align_bytes=64)
         at_s = keep.tile([P, HG, F], U8, name="at_s", align_bytes=64)
         ident = keep.tile([P, P], F32, name="ident", align_bytes=64)
         leak_in = keep.tile([P, HG, PACK], BF16, name="leak_in")
         r_in = keep.tile([P, MG, PACK], BF16, name="r_in")
         leak_col = keep.tile([P, HG, PACK], F32, name="leak_col")
-        oml_col = keep.tile([P, HG, PACK], F32, name="oml_col")
+        rest_col = keep.tile([P, HG, PACK], F32, name="rest_col")
         r_col = keep.tile([P, MG, PACK], F32, name="r_col")
         warm = keep.tile([P, 1], F32, name="warm")
         dyq = keep.tile([P, MG, HG, KP], U32, name="dyq", align_bytes=64)
         dyq_s = keep.tile([P, MG, HG, KP], U8, name="dyq_s", align_bytes=64)
-        d1 = [keep.tile([P, PACK, H], F32, name=f"d1_{g}", align_bytes=64) for g in range(MG)]
+        d1 = keep.tile([P, MG, PACK, H], F32, name="d1", align_bytes=64)
         d1q = keep.tile([P, MG, H], U32, name="d1q", align_bytes=64)
         d1q_s = keep.tile([P, MG, H], U8, name="d1q_s", align_bytes=64)
-        slope = [keep.tile([P, PACK, M], BF16, name=f"slope{f}", align_bytes=64) for f in range(HG)]
+        slope = keep.tile([P, HG, PACK, M], BF16, name="slope", align_bytes=64)
+        dzq = keep.tile([P, HG, M], U32, name="dzq", align_bytes=64)
+        dzq_s = keep.tile([P, HG, M], U8, name="dzq_s", align_bytes=64)
 
         nc.vector.memset(bt_s[:].rearrange("p g n -> p (g n)").bitcast(I32), 0)
         nc.gpsimd.memset(warm[:], 0.0)
         nc.vector.memset(c_in_s[:].rearrange("p g n -> p (g n)").bitcast(I32), 0)
         nc.vector.memset(at_s[:].rearrange("p g n -> p (g n)").bitcast(I32), 0)
         make_identity(nc, ident[:])
-        nc.scalar.activation(out=warm[:], in_=warm[:], func=IDENTITY)
+        nc.scalar.activation(out=warm[:], in_=warm[:], func=ACT.Identity)
 
         dy_v = dy.rearrange("(g p t) h -> g p t h", g=MG, t=PACK)
         z_v = z.rearrange("(g p t) h -> g p t h", g=MG, t=PACK)
@@ -75,81 +73,79 @@ def tile_residual_prelu_layer_backward_t2_kernel(
 
         def load_dy(g, f, t0, t1):
             cols = slice(KP * f, KP * (f + 1))
-            nc.sync.dma_start(out=dy_sb[g][:, t0:t1, cols], in_=dy_v[g][:, t0:t1, cols])
+            nc.sync.dma_start(out=dy_sb[:, g, t0:t1, cols], in_=dy_v[g][:, t0:t1, cols])
 
         def load_words(tile, words, g):
             nc.sync.dma_start(out=tile[:, g, :].bitcast(I32), in_=words[g].bitcast(I32))
 
-        def load_scales(queue, tile, scales):
-            src = scales.bitcast(I32)
+        def load_scales(tile, scales):
+            rows = scales.bitcast(I32)
             for q in range(4):
-                queue.dma_start(
+                nc.sync.dma_start(
                     out=tile[32 * q : 32 * q + 4, :, :].bitcast(I32),
-                    in_=src[:, 4 * q : 4 * q + 4, :].rearrange("g q n -> q g n"),
+                    in_=rows[:, 4 * q : 4 * q + 4, :].rearrange("g q n -> q g n"),
                 )
 
         load_dy(0, 0, 0, 2)
         load_dy(0, 0, 2, 4)
-        load_scales(nc.gpsimd, bt_s, bt_scales)
-        load_dy(0, 1, 0, 4)
+        load_scales(bt_s, bt_scales)
         load_words(bt, bt_words, 0)
-        load_dy(0, 2, 0, 4)
+        load_dy(0, 1, 0, 4)
         load_words(bt, bt_words, 1)
+        load_dy(0, 2, 0, 4)
         load_words(bt, bt_words, 2)
-        load_scales(nc.sync, c_in_s, c_scales)
-        for g in range(MG):
-            load_words(c_in, c_words, g)
         nc.gpsimd.dma_start(out=leak_in[:], in_=leak.rearrange("(f p t) -> p f t", f=HG, t=PACK))
         nc.gpsimd.dma_start(out=r_in[:], in_=r.rearrange("(g p t) -> p g t", g=MG, t=PACK))
-        load_dy(1, 0, 0, 4)
-        load_dy(1, 1, 0, 4)
-        load_dy(1, 2, 0, 4)
-        nc.sync.dma_start(out=z_sb[0][:], in_=z_v[0])
-        nc.sync.dma_start(out=z_sb[1][:], in_=z_v[1])
-        load_scales(nc.sync, at_s, at_scales)
+        for f in range(HG):
+            load_dy(1, f, 0, 4)
+        load_scales(c_in_s, c_scales)
+        for g in range(MG):
+            load_words(c_in, c_words, g)
+        for g in range(MG):
+            nc.sync.dma_start(out=z_sb[:, g, :, :], in_=z_v[g])
+        load_scales(at_s, at_scales)
         for f in range(HG):
             load_words(at, at_words, f)
 
-        def dy_transposes(g, f):
-            words = dy_sb[g][:].rearrange("p t h -> p (t h)").bitcast(F32).rearrange("p (t w) -> p t w", t=PACK)
-            banks = []
-            for half in range(2):
-                tr = ps_tr.tile([P, 2, 2 * P], F32, name="tr")
-                for j in range(2):
-                    for u in range(2):
-                        lo = KP // 2 * f + u
-                        nc.tensor.transpose(
-                            tr[:, u, P * j : P * (j + 1)], words[:, 2 * half + j, lo : KP // 2 * (f + 1) : 2], ident[:]
-                        )
-                banks.append(tr)
-            return banks
+        nc.gpsimd.tensor_copy(out=leak_col[:], in_=leak_in[:])
+        nc.gpsimd.tensor_scalar(
+            out=rest_col[:], in0=leak_in[:], scalar1=-1.0, scalar2=1.0, op0=ALU.mult, op1=ALU.add
+        )
+        nc.gpsimd.tensor_copy(out=r_col[:], in_=r_in[:])
 
-        def dy_copy_quant(g, f, banks, engines):
-            tiles = []
-            for half in range(2):
-                dyt = stage.tile([P, 2 * P, PACK], BF16, name="dyt", bufs=6, align_bytes=64)
-                dst = dyt[:].rearrange("p m j -> p (m j)").bitcast(F32).rearrange("p (m u) -> p m u", u=2)
-                src = banks[half][:].rearrange("p u m -> p m u")
-                if engines[half] == "s":
-                    nc.scalar.copy(out=dst, in_=src)
-                else:
-                    nc.vector.tensor_copy(out=dst, in_=src)
-                tiles.append(dyt)
-            return tiles
+        dy_words = dy_sb[:].rearrange("p g t h -> p (g t h)").bitcast(F32).rearrange("p (g t w) -> p g t w", g=MG, t=PACK)
+        turned_dy, grouped_dy, acc1, grouped_d1 = {}, {}, {}, {}
 
-        def dy_quant(g, f, tiles):
-            for half in range(2):
-                cols = slice(2 * P * half, 2 * P * (half + 1))
-                nc.vector.quantize_mx(
-                    out=dyq[:, g, f, cols].bitcast(FP8X4),
-                    scales=dyq_s[:, g, f, cols],
-                    in_=tiles[half][:].rearrange("p m j -> p (m j)"),
-                )
+        def turn_dy(g, f, half):
+            turned = ps_tr.tile([P, 2, 2 * P], F32, name="turned")
+            for j in range(2):
+                for u in range(2):
+                    lo, hi = KP // 2 * f + u, KP // 2 * (f + 1)
+                    nc.tensor.transpose(
+                        turned[:, u, P * j : P * (j + 1)], dy_words[:, g, 2 * half + j, lo:hi:2], ident[:]
+                    )
+            turned_dy[g, f, half] = turned
 
-        def mx1(acc, g, n, t, f):
+        def group_dy(g, f, half):
+            dyt = stage.tile([P, 2 * P, PACK], BF16, name="dyt", bufs=4, align_bytes=64)
+            dst = dyt[:].rearrange("p m j -> p (m j)").bitcast(F32).rearrange("p (m u) -> p m u", u=2)
+            nc.scalar.copy(out=dst, in_=turned_dy[g, f, half][:].rearrange("p u m -> p m u"))
+            grouped_dy[g, f, half] = dyt
+
+        def quantize_dy(g, f, half):
+            cols = slice(2 * P * half, 2 * P * (half + 1))
+            nc.vector.quantize_mx(
+                out=dyq[:, g, f, cols].bitcast(FP8X4),
+                scales=dyq_s[:, g, f, cols],
+                in_=grouped_dy[g, f, half][:].rearrange("p m j -> p (m j)"),
+            )
+
+        def stage1_pass(g, n, t, f):
+            if f == 0:
+                acc1[g, n, t] = ps_acc.tile([P, KP], F32, name="acc")
             rows = slice(P * t, P * (t + 1))
             nc.tensor.matmul_mx(
-                out=acc[:],
+                out=acc1[g, n, t][:],
                 lhsT=dyq[:, g, f, rows].bitcast(FP8X4),
                 lhsT_scale=dyq_s[:, g, f, rows],
                 rhs=bt[:, f, 2 * KP * n : 2 * KP * (n + 1)].bitcast(FP4X4),
@@ -158,283 +154,207 @@ def tile_residual_prelu_layer_backward_t2_kernel(
                 stop=(f == HG - 1),
             )
 
-        def add_dy(acc, g, n, t):
+        def stage1_passes(g, n, t):
+            for f in range(HG):
+                stage1_pass(g, n, t, f)
+
+        def add_dy(g, n, t):
             cols = slice(KP * n, KP * (n + 1))
             nc.vector.tensor_tensor(
-                out=d1[g][:, t, cols].rearrange("p (k q) -> p k q", k=PACK),
-                in0=acc[:].rearrange("p (q k) -> p k q", k=PACK),
-                in1=dy_sb[g][:, t, cols].rearrange("p (q k) -> p k q", k=PACK),
-                op=ADD,
+                out=d1[:, g, t, cols].rearrange("p (k q) -> p k q", k=PACK),
+                in0=acc1[g, n, t][:].rearrange("p (q k) -> p k q", k=PACK),
+                in1=dy_sb[:, g, t, cols].rearrange("p (q k) -> p k q", k=PACK),
+                op=ALU.add,
             )
 
-        def unit1(g, n, t):
-            acc = ps_mm.tile([P, KP], F32, name="acc")
-            for f in range(HG):
-                mx1(acc, g, n, t, f)
-            add_dy(acc, g, n, t)
+        def round_d1(g, n):
+            d1t = stage.tile([P, KP, PACK], BF16, name="d1t", bufs=2, align_bytes=64)
+            nc.scalar.copy(out=d1t[:], in_=d1[:, g, :, KP * n : KP * (n + 1)].rearrange("p t c -> p c t"))
+            grouped_d1[g, n] = d1t
 
-        grouped = {}
-
-        def interleave_d1(g, n, parts):
-            d1t = stage.tile([P, KP, PACK], BF16, name="d1t", bufs=3, align_bytes=64)
-            grouped[g, n] = d1t
-            for eng, c0, c1 in parts:
-                src = d1[g][:, :, KP * n + c0 : KP * n + c1].rearrange("p t c -> p c t")
-                if eng == "s":
-                    nc.scalar.copy(out=d1t[:, c0:c1, :], in_=src)
-                else:
-                    nc.vector.tensor_copy(out=d1t[:, c0:c1, :], in_=src)
-
-        def quant_d1(g, n):
+        def quantize_d1(g, n):
             cols = slice(KP * n, KP * (n + 1))
             nc.vector.quantize_mx(
                 out=d1q[:, g, cols].bitcast(FP8X4),
                 scales=d1q_s[:, g, cols],
-                in_=grouped[g, n][:].rearrange("p c t -> p (c t)"),
+                in_=grouped_d1[g, n][:].rearrange("p c t -> p (c t)"),
             )
 
-        def scale_d1(g, t, eng):
-            if eng == "s":
-                nc.scalar.activation(out=d1[g][:, t, :], in_=d1[g][:, t, :], func=COPY, scale=r_col[:, g, t : t + 1])
-            else:
-                for n in range(HG):
-                    cols = slice(KP * n, KP * (n + 1))
-                    nc.gpsimd.tensor_scalar(
-                        out=d1[g][:, t, cols], in0=d1[g][:, t, cols],
-                        scalar1=r_col[:, g, t : t + 1], scalar2=0.0, op0=MULT, op1=ADD,
-                    )
+        def scale_d1(j, f):
+            g, t = divmod(j, PACK)
+            part = d1[:, g, t, KP * f : KP * (f + 1)]
+            nc.scalar.activation(out=part, in_=part, func=ACT.Copy, scale=r_col[:, g, t : t + 1])
 
-        mask = {}
+        def order_c_words(gk, g):
+            cols = slice(2 * KP * g, 2 * KP * (g + 1))
+            nc.vector.tensor_copy(
+                out=c[:, gk, cols].rearrange("p (t m b) -> p t m b", t=PACK, b=2),
+                in_=c_in[:, gk, cols].rearrange("p (m t b) -> p t m b", t=PACK, b=2),
+            )
 
-        def make_mask(g, t):
-            if t == 0:
-                mask[g] = keep.tile([P, PACK, 2, H // 2], BF16, name=f"mask{g}", tag="rows" if g == 0 else "zrows", bufs=MG, align_bytes=64)
+        def order_c_scales(gk):
+            nc.vector.tensor_copy(
+                out=c_s[:, gk, :].rearrange("p (g t m) -> p g t m", g=MG, t=PACK),
+                in_=c_in_s[:, gk, :].rearrange("p (g m t) -> p g t m", g=MG, t=PACK),
+            )
+
+        mask_of, turned_mask = {}, {}
+
+        def make_mask(g, f, u):
+            mask = stage.tile([P, PACK, P, 2], BF16, name="mask", bufs=3, align_bytes=64)
+            z_part = z_sb[:, g, :, KP * f : KP * (f + 1)].rearrange("p t (q u e) -> p u t q e", u=2, e=2)
             nc.vector.tensor_scalar(
-                out=mask[g][:, t, :, :].rearrange("p u (q e) -> p u q e", e=2),
-                in0=z_sb[g][:, t, :].rearrange("p (q u e) -> p u q e", u=2, e=2),
-                scalar1=0.0, scalar2=None, op0=IS_GT,
+                out=mask[:], in0=z_part[:, u, :, :, :], scalar1=0.0, scalar2=None, op0=ALU.is_gt
             )
+            mask_of[g, f, u] = mask
 
-        def mask_transposes(g, f, u):
-            words = mask[g][:].rearrange("p t u c -> p (t u c)").bitcast(F32).rearrange("p (t u w) -> p t u w", t=PACK, u=2)
-            tr = ps_tr.tile([P, PACK, P], F32, name="tr")
+        def turn_mask(g, f, u):
+            words = mask_of[g, f, u][:].rearrange("p t q e -> p (t q e)").bitcast(F32)
+            turned = ps_tr.tile([P, PACK, P], F32, name="turned")
             for t in range(PACK):
-                nc.tensor.transpose(tr[:, t, :], words[:, t, u, P * f : P * (f + 1)], ident[:])
-            return tr
+                nc.tensor.transpose(turned[:, t, :], words[:, P * t : P * (t + 1)], ident[:])
+            turned_mask[g, f, u] = turned
 
-        def make_slope(g, f, u, tr):
-            pairs = tr[:].rearrange("p t m -> p (t m)").bitcast(BF16)
+        def make_slope(g, f, u):
+            pairs = turned_mask[g, f, u][:].rearrange("p t m -> p (t m)").bitcast(BF16)
             for e in range(2):
                 k = 2 * u + e
                 nc.scalar.activation(
-                    out=slope[f][:, k, KP * g : KP * (g + 1)],
+                    out=slope[:, f, k, KP * g : KP * (g + 1)],
                     in_=pairs[:, e : 2 * KP : 2],
-                    func=IDENTITY,
+                    func=ACT.Identity,
                     bias=leak_col[:, f, k : k + 1],
-                    scale=oml_col[:, f, k : k + 1],
+                    scale=rest_col[:, f, k : k + 1],
                 )
 
-        def mask_unit(g, f, u):
-            make_slope(g, f, u, mask_transposes(g, f, u))
+        acc2, v_of, turned_of, dz_of = {}, {}, {}, {}
 
-        def permute_c(gk, gm):
-            a, b = 2 * KP * gm, 2 * KP * (gm + 1)
-            nc.vector.tensor_copy(
-                out=cp[:, gk, a:b].rearrange("p (t m b) -> p t m b", t=PACK, b=2),
-                in_=c_in[:, gk, a:b].rearrange("p (m t b) -> p t m b", t=PACK, b=2),
-            )
-
-        def permute_c_scales(gk, gm):
-            a, b = KP * gm, KP * (gm + 1)
-            nc.vector.tensor_copy(
-                out=cp_s[:, gk, a:b].rearrange("p (t m) -> p t m", t=PACK),
-                in_=c_in_s[:, gk, a:b].rearrange("p (m t) -> p t m", t=PACK),
-            )
-
-        accs, vs, vts, dzs, dzqs = {}, {}, {}, {}, {}
-
-        def mx2(j, f):
-            g, t = divmod(j, PACK)
-            acc = ps_mm.tile([P, KP], F32, name="acc")
-            lo = KP * g + P * t
+        def stage2_passes(j, f):
+            acc = ps_acc.tile([P, KP], F32, name="acc")
             for gk in range(MG):
                 nc.tensor.matmul_mx(
                     out=acc[:],
-                    lhsT=cp[:, gk, 2 * lo : 2 * (lo + P)].bitcast(FP4X4),
-                    lhsT_scale=cp_s[:, gk, lo : lo + P],
+                    lhsT=c[:, gk, 2 * P * j : 2 * P * (j + 1)].bitcast(FP4X4),
+                    lhsT_scale=c_s[:, gk, P * j : P * (j + 1)],
                     rhs=d1q[:, gk, KP * f : KP * (f + 1)].bitcast(FP8X4),
                     rhs_scale=d1q_s[:, gk, KP * f : KP * (f + 1)],
                     start=(gk == 0),
                     stop=(gk == MG - 1),
                 )
-            accs[j, f] = acc
+            acc2[j, f] = acc
 
-        def finish_d2(j, f):
+        def make_v(j, f):
             g, t = divmod(j, PACK)
-            v = stage.tile([P, KP], F32, name="v", bufs=8, align_bytes=64)
+            v = stage.tile([P, KP], F32, name="v", bufs=4, align_bytes=64)
             nc.vector.scalar_tensor_tensor(
-                out=v[:], in0=accs[j, f][:], scalar=r_col[:, g, t : t + 1],
-                in1=d1[g][:, t, KP * f : KP * (f + 1)], op0=MULT, op1=ADD,
+                out=v[:], in0=acc2[j, f][:], scalar=r_col[:, g, t : t + 1],
+                in1=d1[:, g, t, KP * f : KP * (f + 1)], op0=ALU.mult, op1=ALU.add,
             )
-            vs[j, f] = v
+            v_of[j, f] = v
 
-        def v_transposes(j, f):
-            vt = ps_tr.tile([P, PACK, P], F32, name="tr")
+        def turn_v(j, f):
+            turned = ps_tr.tile([P, PACK, P], F32, name="turned")
             for k in range(PACK):
-                nc.tensor.transpose(vt[:, k, :], vs[j, f][:, P * k : P * (k + 1)], ident[:])
-            vts[j, f] = vt
+                nc.tensor.transpose(turned[:, k, :], v_of[j, f][:, P * k : P * (k + 1)], ident[:])
+            turned_of[j, f] = turned
 
         def make_dz(j, f):
-            dz = stage.tile([P, P, PACK], BF16, name="dz", bufs=6, align_bytes=64)
+            if j % PAIR == 0:
+                dz_of[j // PAIR, f] = stage.tile([P, PAIR, P, PACK], BF16, name="dz", bufs=2, align_bytes=64)
             nc.vector.tensor_tensor(
-                out=dz[:],
-                in0=vts[j, f][:].rearrange("p k m -> p m k"),
-                in1=slope[f][:, :, P * j : P * (j + 1)].rearrange("p k m -> p m k"),
-                op=MULT,
+                out=dz_of[j // PAIR, f][:, j % PAIR, :, :],
+                in0=turned_of[j, f][:].rearrange("p k m -> p m k"),
+                in1=slope[:, f, :, P * j : P * (j + 1)].rearrange("p k m -> p m k"),
+                op=ALU.mult,
             )
-            dzs[j, f] = dz
 
-        def quant_dz(j, f):
-            codes = stage.tile([P, P], U32, name="dzq", bufs=9, align_bytes=64)
-            scales = stage.tile([P, P], U8, name="dzq_s", bufs=9, align_bytes=64)
+        def quantize_dz(jp, f, a, b):
+            cols = slice(P * (PAIR * jp + a), P * (PAIR * jp + b))
             nc.vector.quantize_mx(
-                out=codes[:].bitcast(FP8X4), scales=scales[:], in_=dzs[j, f][:].rearrange("p m k -> p (m k)")
+                out=dzq[:, f, cols].bitcast(FP8X4),
+                scales=dzq_s[:, f, cols],
+                in_=dz_of[jp, f][:, a:b, :, :].rearrange("p i m k -> p (i m k)"),
             )
-            dzqs[j, f] = (codes, scales)
 
-        def mx3(j):
-            po = ps_out.tile([P, F], F32, name="po")
+        acc3 = {}
+
+        def stage3_passes(j):
+            acc = ps_acc.tile([P, F], F32, name="acc")
             for f in range(HG):
-                codes, scales = dzqs[j, f]
                 nc.tensor.matmul_mx(
-                    out=po[:],
-                    lhsT=codes[:].bitcast(FP8X4),
-                    lhsT_scale=scales[:],
+                    out=acc[:],
+                    lhsT=dzq[:, f, P * j : P * (j + 1)].bitcast(FP8X4),
+                    lhsT_scale=dzq_s[:, f, P * j : P * (j + 1)],
                     rhs=at[:, f, :].bitcast(FP4X4),
                     rhs_scale=at_s[:, f, :],
                     start=(f == 0),
                     stop=(f == HG - 1),
                 )
-            return po
+            acc3[j] = acc
 
-        def store(j, po):
+        def store(j):
             g, t = divmod(j, PACK)
-            res = stage.tile([P, F], F32, name="res", bufs=3, align_bytes=64)
-            nc.scalar.copy(out=res[:], in_=po[:])
+            res = stage.tile([P, F], F32, name="res", bufs=4, align_bytes=64)
+            nc.scalar.copy(out=res[:], in_=acc3[j][:])
             nc.sync.dma_start(out=out_v[g][:, t, :], in_=res[:])
 
-        b00 = dy_copy_quant(0, 0, dy_transposes(0, 0), "sv")
-        dy_quant(0, 0, b00)
-        b01 = dy_copy_quant(0, 1, dy_transposes(0, 1), "ss")
-        dy_quant(0, 1, b01)
-        nc.gpsimd.tensor_copy(out=leak_col[:], in_=leak_in[:])
-        nc.gpsimd.tensor_scalar(out=oml_col[:], in0=leak_in[:], scalar1=-1.0, scalar2=1.0, op0=MULT, op1=ADD)
-        nc.gpsimd.tensor_copy(out=r_col[:], in_=r_in[:])
-        first = [ps_mm.tile([P, KP], F32, name="acc") for t in range(PACK)]
-        for t in range(PACK):
-            mx1(first[t], 0, 0, t, 0)
-        b02 = dy_copy_quant(0, 2, dy_transposes(0, 2), "ss")
-        dy_quant(0, 2, b02)
-        for t in range(PACK):
-            mx1(first[t], 0, 0, t, 1)
-        for t in range(PACK):
-            mx1(first[t], 0, 0, t, 2)
-            add_dy(first[t], 0, 0, t)
-        interleave_d1(0, 0, [("s", 0, KP)])
-        unit1(0, 1, 0)
-        permute_c(0, 0)
-        unit1(0, 1, 1)
-        permute_c(1, 0)
-        permute_c_scales(0, 0)
-        b10 = dy_copy_quant(1, 0, dy_transposes(1, 0), "ss")
-        unit1(0, 1, 2)
-        quant_d1(0, 0)
-        unit1(0, 1, 3)
-        permute_c_scales(1, 0)
-        permute_c(0, 1)
-        dy_quant(1, 0, b10)
-        interleave_d1(0, 1, [("s", 0, KP)])
-        unit1(0, 2, 0)
-        b11 = dy_copy_quant(1, 1, dy_transposes(1, 1), "ss")
-        unit1(0, 2, 1)
-        permute_c(1, 1)
-        quant_d1(0, 1)
-        unit1(0, 2, 2)
-        dy_quant(1, 1, b11)
-        for gk in range(MG):
-            permute_c_scales(gk, 1)
-        b12 = dy_copy_quant(1, 2, dy_transposes(1, 2), "ss")
-        unit1(0, 2, 3)
-        interleave_d1(0, 2, [("s", 0, KP)])
-        dy_quant(1, 2, b12)
-        make_mask(0, 0)
-        make_mask(0, 1)
-        unit1(1, 0, 0)
-        unit1(1, 0, 1)
-        make_mask(0, 2)
-        make_mask(0, 3)
-        unit1(1, 0, 2)
-        unit1(1, 0, 3)
-        quant_d1(0, 2)
-        mask_unit(0, 0, 0)
-        mask_unit(0, 0, 1)
-        interleave_d1(1, 0, [("s", 0, KP)])
-        unit1(1, 1, 0)
-        unit1(1, 1, 1)
-        make_mask(1, 0)
-        make_mask(1, 1)
-        unit1(1, 1, 2)
-        quant_d1(1, 0)
-        mask_unit(0, 1, 0)
-        mask_unit(0, 1, 1)
-        unit1(1, 1, 3)
-        interleave_d1(1, 1, [("s", 0, KP)])
-        make_mask(1, 2)
-        make_mask(1, 3)
-        unit1(1, 2, 0)
-        mask_unit(0, 2, 0)
-        unit1(1, 2, 1)
-        unit1(1, 2, 2)
-        quant_d1(1, 1)
-        unit1(1, 2, 3)
-        scale_d1(0, 0, "s")
-        mx2(0, 0)
-        mx2(0, 1)
-        interleave_d1(1, 2, [("s", 0, 208), ("v", 208, KP)])
-        scale_d1(0, 1, "s")
-        mask_unit(0, 2, 1)
-        finish_d2(0, 0)
-        mx2(1, 0)
-        quant_d1(1, 2)
+        blocks = [(0, 0), (0, 1), (1, 0), (1, 1), (0, 2), (1, 2)]
+        plan = []
 
-        units = [(0, 0), (0, 1), (1, 0), (1, 1), (0, 2), (1, 2)]
-        units += [(j, f) for j in range(2, M // P) for f in range(HG)]
-        groups = [units[i : i + 3] for i in range(0, len(units), 3)]
-        pe_extra = {1: [(1, 0, 0)], 2: [(1, 0, 1), (1, 1, 0)], 3: [(1, 1, 1)], 4: [(1, 2, 0), (1, 2, 1)]}
-        ready = {3: 1, 4: 2, 5: 3, 6: 4, 7: 5, 8: 6, 9: 7}
-        s_scale = {0: [2], 1: [3], 2: [4], 3: [5], 4: [6], 5: [7]}
-        for i in range(len(groups) + 2):
-            now = groups[i] if i < len(groups) else []
-            prev = groups[i - 1] if 1 <= i <= len(groups) else []
-            if i > 0:
-                for j, f in now:
-                    mx2(j, f)
-            for j, f in prev:
-                v_transposes(j, f)
-            if i == 3:
-                store(0, mx3(0))
-            for args in pe_extra.get(i, []):
-                mask_unit(*args)
-            for x in range(3):
-                if now and (i > 0 or x > 0):
-                    finish_d2(*now[x])
-                if prev:
-                    make_dz(*prev[x])
-                    if x > 0:
-                        quant_dz(*prev[x - 1])
-            if prev:
-                quant_dz(*prev[2])
-            if i in ready:
-                store(ready[i], mx3(ready[i]))
-            for j in s_scale.get(i, []):
-                scale_d1(j // PACK, j % PACK, "s")
+        def at_tick(tick, step, *args):
+            plan.append((tick, step, args))
+
+        dy_tick = {(0, 0): 2, (0, 1): 14, (0, 2): 20, (1, 0): 41, (1, 1): 49, (1, 2): 55}
+        halves = [(g, f, half) for g in range(MG) for f in range(HG) for half in range(2)]
+        for g, f, half in halves:
+            at_tick(dy_tick[g, f] + 1 * half, turn_dy, g, f, half)
+        for g, f, half in halves:
+            at_tick(dy_tick[g, f] + 1 * half, group_dy, g, f, half)
+        for g, f, half in halves:
+            at_tick(dy_tick[g, f] + 1 * half + (6, 11)[g], quantize_dy, g, f, half)
+        for f in range(HG):
+            for t in range(PACK):
+                at_tick((10, 26, 33)[f], stage1_pass, 0, 0, t, f)
+        block_tick = (45, 58, 109, 145, 187, 169)
+        add_tick = {}
+        for b in range(1, len(blocks)):
+            for t in range(PACK):
+                at_tick(block_tick[b] + 3 * t, stage1_passes, *blocks[b], t)
+        for b in range(len(blocks)):
+            for t in range(PACK):
+                add_tick[b] = block_tick[b] + (t if b == 0 else 3 * t + 20)
+                at_tick(add_tick[b], add_dy, *blocks[b], t)
+        for b in range(len(blocks)):
+            at_tick(add_tick[b] + 22, round_d1, *blocks[b])
+        for b in range(len(blocks)):
+            at_tick(add_tick[b] + 51, quantize_d1, *blocks[b])
+        for g in range(MG):
+            for gk in range(MG):
+                at_tick((61, 137)[g] + 2 * gk, order_c_words, gk, g)
+        for gk in range(MG):
+            at_tick(157 + 2 * gk, order_c_scales, gk)
+        units = [(j, f) for f in range(HG) for j in range(M // P)]
+        chunk_tick = (206, 240, 268)
+        mask_tick = {(0, 0): 129, (1, 0): 207, (0, 1): 115, (1, 1): 229, (0, 2): 241, (1, 2): 255}
+        parts = [(g, f, u) for g in range(MG) for f in range(HG) for u in range(2)]
+        for j, f in units:
+            at_tick(chunk_tick[f] + 4 * j + (-1), scale_d1, j, f)
+        for lag, step in ((0, make_mask), (14, turn_mask), (17, make_slope)):
+            for g, f, u in parts:
+                at_tick(mask_tick[g, f] + 7 * u + lag, step, g, f, u)
+        for lag, step in ((0, stage2_passes), (11, make_v), (12, turn_v), (19, make_dz)):
+            for j, f in units:
+                at_tick(chunk_tick[f] + 4 * j + lag, step, j, f)
+        for f in range(HG):
+            for jp in range(M // P // PAIR):
+                tick = chunk_tick[f] + 4 * (PAIR * jp + 1) + 24
+                if f < HG - 1 or jp < M // P // PAIR - 1:
+                    at_tick(tick, quantize_dz, jp, f, 0, PAIR)
+        for i in range(PAIR):
+            at_tick(chunk_tick[2] + 4 * (M // P - PAIR + i) + 24, quantize_dz, M // P // PAIR - 1, 2, i, i + 1)
+        for step in (stage3_passes, store):
+            for j in range(M // P):
+                last = j if j >= M // P - PAIR else PAIR * (j // PAIR) + 1
+                at_tick(chunk_tick[2] + 4 * last + 24, step, j)
+        for tick, step, args in sorted(plan, key=lambda entry: entry[0]):
+            step(*args)

from contextlib import ExitStack

import concourse.mybir as mybir
from concourse.masks import make_identity

F32 = mybir.dt.float32
BF16 = mybir.dt.bfloat16
I32 = mybir.dt.int32
U32 = mybir.dt.uint32
U8 = mybir.dt.uint8
FP8X4 = mybir.dt.float8_e4m3fn_x4
FP4X4 = mybir.dt.float4_e2m1fn_x4
ALU = mybir.AluOpType
ACT = mybir.ActivationFunctionType

M, H, F = 1024, 1536, 512
P = 128
PACK = 4
KP = P * PACK
MG = M // KP
HG = H // KP
PAIR = 2

FLOPS = 2 * M * H * H + 2 * M * M * H + 2 * M * H * F


def tile_residual_prelu_layer_backward_t2_kernel(
    tc, dy, z, leak, r, bt_words, bt_scales, c_words, c_scales, at_words, at_scales, out
):
    nc = tc.nc
    with ExitStack() as ctx:
        keep = ctx.enter_context(tc.tile_pool(name="keep", bufs=1))
        stage = ctx.enter_context(tc.tile_pool(name="stage", bufs=2))
        ps_acc = ctx.enter_context(tc.psum_pool(name="ps_acc", bufs=5))
        ps_tr = ctx.enter_context(tc.psum_pool(name="ps_tr", bufs=3))
        ctx.enter_context(tc.manual_schedule())
        dy_sb = keep.tile([P, MG, PACK, H], BF16, name="dy_sb", align_bytes=64)
        z_sb = keep.tile([P, MG, PACK, H], BF16, name="z_sb", align_bytes=64)
        bt = keep.tile([P, HG, 2 * H], U8, name="bt", align_bytes=64)
        bt_s = keep.tile([P, HG, H], U8, name="bt_s", align_bytes=64)
        c_in = keep.tile([P, MG, 2 * M], U8, name="c_in", align_bytes=64)
        c_in_s = keep.tile([P, MG, M], U8, name="c_in_s", align_bytes=64)
        c = keep.tile([P, MG, 2 * M], U8, name="c", align_bytes=64)
        c_s = keep.tile([P, MG, M], U8, name="c_s", align_bytes=64)
        at = keep.tile([P, HG, 2 * F], U8, name="at", align_bytes=64)
        at_s = keep.tile([P, HG, F], U8, name="at_s", align_bytes=64)
        ident = keep.tile([P, P], F32, name="ident", align_bytes=64)
        leak_in = keep.tile([P, HG, PACK], BF16, name="leak_in")
        r_in = keep.tile([P, MG, PACK], BF16, name="r_in")
        leak_col = keep.tile([P, HG, PACK], F32, name="leak_col")
        rest_col = keep.tile([P, HG, PACK], F32, name="rest_col")
        r_col = keep.tile([P, MG, PACK], F32, name="r_col")
        warm = keep.tile([P, 1], F32, name="warm")
        dyq = keep.tile([P, MG, HG, KP], U32, name="dyq", align_bytes=64)
        dyq_s = keep.tile([P, MG, HG, KP], U8, name="dyq_s", align_bytes=64)
        d1 = keep.tile([P, MG, PACK, H], F32, name="d1", align_bytes=64)
        d1q = keep.tile([P, MG, H], U32, name="d1q", align_bytes=64)
        d1q_s = keep.tile([P, MG, H], U8, name="d1q_s", align_bytes=64)
        slope = keep.tile([P, HG, PACK, M], BF16, name="slope", align_bytes=64)
        dzq = keep.tile([P, HG, M], U32, name="dzq", align_bytes=64)
        dzq_s = keep.tile([P, HG, M], U8, name="dzq_s", align_bytes=64)

        nc.vector.memset(bt_s[:].rearrange("p g n -> p (g n)").bitcast(I32), 0)
        nc.gpsimd.memset(warm[:], 0.0)
        nc.vector.memset(c_in_s[:].rearrange("p g n -> p (g n)").bitcast(I32), 0)
        nc.vector.memset(at_s[:].rearrange("p g n -> p (g n)").bitcast(I32), 0)
        make_identity(nc, ident[:])
        nc.scalar.activation(out=warm[:], in_=warm[:], func=ACT.Identity)

        dy_v = dy.rearrange("(g p t) h -> g p t h", g=MG, t=PACK)
        z_v = z.rearrange("(g p t) h -> g p t h", g=MG, t=PACK)
        out_v = out.rearrange("(g p t) n -> g p t n", g=MG, t=PACK)

        def load_dy(g, f, t0, t1):
            cols = slice(KP * f, KP * (f + 1))
            nc.sync.dma_start(out=dy_sb[:, g, t0:t1, cols], in_=dy_v[g][:, t0:t1, cols])

        def load_words(tile, words, g):
            nc.sync.dma_start(out=tile[:, g, :].bitcast(I32), in_=words[g].bitcast(I32))

        def load_scales(tile, scales):
            rows = scales.bitcast(I32)
            for q in range(4):
                nc.sync.dma_start(
                    out=tile[32 * q : 32 * q + 4, :, :].bitcast(I32),
                    in_=rows[:, 4 * q : 4 * q + 4, :].rearrange("g q n -> q g n"),
                )

        load_dy(0, 0, 0, 2)
        load_dy(0, 0, 2, 4)
        load_scales(bt_s, bt_scales)
        load_words(bt, bt_words, 0)
        load_dy(0, 1, 0, 4)
        load_words(bt, bt_words, 1)
        load_dy(0, 2, 0, 4)
        load_words(bt, bt_words, 2)
        nc.gpsimd.dma_start(out=leak_in[:], in_=leak.rearrange("(f p t) -> p f t", f=HG, t=PACK))
        nc.gpsimd.dma_start(out=r_in[:], in_=r.rearrange("(g p t) -> p g t", g=MG, t=PACK))
        for f in range(HG):
            load_dy(1, f, 0, 4)
        load_scales(c_in_s, c_scales)
        for g in range(MG):
            load_words(c_in, c_words, g)
        for g in range(MG):
            nc.sync.dma_start(out=z_sb[:, g, :, :], in_=z_v[g])
        load_scales(at_s, at_scales)
        for f in range(HG):
            load_words(at, at_words, f)

        nc.gpsimd.tensor_copy(out=leak_col[:], in_=leak_in[:])
        nc.gpsimd.tensor_scalar(
            out=rest_col[:], in0=leak_in[:], scalar1=-1.0, scalar2=1.0, op0=ALU.mult, op1=ALU.add
        )
        nc.gpsimd.tensor_copy(out=r_col[:], in_=r_in[:])

        dy_words = dy_sb[:].rearrange("p g t h -> p (g t h)").bitcast(F32).rearrange("p (g t w) -> p g t w", g=MG, t=PACK)
        turned_dy, grouped_dy, acc1, grouped_d1 = {}, {}, {}, {}

        def turn_dy(g, f, half):
            turned = ps_tr.tile([P, 2, 2 * P], F32, name="turned")
            for j in range(2):
                for u in range(2):
                    lo, hi = KP // 2 * f + u, KP // 2 * (f + 1)
                    nc.tensor.transpose(
                        turned[:, u, P * j : P * (j + 1)], dy_words[:, g, 2 * half + j, lo:hi:2], ident[:]
                    )
            turned_dy[g, f, half] = turned

        def group_dy(g, f, half):
            dyt = stage.tile([P, 2 * P, PACK], BF16, name="dyt", bufs=4, align_bytes=64)
            dst = dyt[:].rearrange("p m j -> p (m j)").bitcast(F32).rearrange("p (m u) -> p m u", u=2)
            nc.scalar.copy(out=dst, in_=turned_dy[g, f, half][:].rearrange("p u m -> p m u"))
            grouped_dy[g, f, half] = dyt

        def quantize_dy(g, f, half):
            cols = slice(2 * P * half, 2 * P * (half + 1))
            nc.vector.quantize_mx(
                out=dyq[:, g, f, cols].bitcast(FP8X4),
                scales=dyq_s[:, g, f, cols],
                in_=grouped_dy[g, f, half][:].rearrange("p m j -> p (m j)"),
            )

        def stage1_pass(g, n, t, f):
            if f == 0:
                acc1[g, n, t] = ps_acc.tile([P, KP], F32, name="acc")
            rows = slice(P * t, P * (t + 1))
            nc.tensor.matmul_mx(
                out=acc1[g, n, t][:],
                lhsT=dyq[:, g, f, rows].bitcast(FP8X4),
                lhsT_scale=dyq_s[:, g, f, rows],
                rhs=bt[:, f, 2 * KP * n : 2 * KP * (n + 1)].bitcast(FP4X4),
                rhs_scale=bt_s[:, f, KP * n : KP * (n + 1)],
                start=(f == 0),
                stop=(f == HG - 1),
            )

        def stage1_passes(g, n, t):
            for f in range(HG):
                stage1_pass(g, n, t, f)

        def add_dy(g, n, t):
            cols = slice(KP * n, KP * (n + 1))
            nc.vector.tensor_tensor(
                out=d1[:, g, t, cols].rearrange("p (k q) -> p k q", k=PACK),
                in0=acc1[g, n, t][:].rearrange("p (q k) -> p k q", k=PACK),
                in1=dy_sb[:, g, t, cols].rearrange("p (q k) -> p k q", k=PACK),
                op=ALU.add,
            )

        def round_d1(g, n):
            d1t = stage.tile([P, KP, PACK], BF16, name="d1t", bufs=2, align_bytes=64)
            nc.scalar.copy(out=d1t[:], in_=d1[:, g, :, KP * n : KP * (n + 1)].rearrange("p t c -> p c t"))
            grouped_d1[g, n] = d1t

        def quantize_d1(g, n):
            cols = slice(KP * n, KP * (n + 1))
            nc.vector.quantize_mx(
                out=d1q[:, g, cols].bitcast(FP8X4),
                scales=d1q_s[:, g, cols],
                in_=grouped_d1[g, n][:].rearrange("p c t -> p (c t)"),
            )

        def scale_d1(j, f):
            g, t = divmod(j, PACK)
            part = d1[:, g, t, KP * f : KP * (f + 1)]
            nc.scalar.activation(out=part, in_=part, func=ACT.Copy, scale=r_col[:, g, t : t + 1])

        def order_c_words(gk, g):
            cols = slice(2 * KP * g, 2 * KP * (g + 1))
            nc.vector.tensor_copy(
                out=c[:, gk, cols].rearrange("p (t m b) -> p t m b", t=PACK, b=2),
                in_=c_in[:, gk, cols].rearrange("p (m t b) -> p t m b", t=PACK, b=2),
            )

        def order_c_scales(gk):
            nc.vector.tensor_copy(
                out=c_s[:, gk, :].rearrange("p (g t m) -> p g t m", g=MG, t=PACK),
                in_=c_in_s[:, gk, :].rearrange("p (g m t) -> p g t m", g=MG, t=PACK),
            )

        mask_of, turned_mask = {}, {}

        def make_mask(g, f, u):
            mask = stage.tile([P, PACK, P, 2], BF16, name="mask", bufs=3, align_bytes=64)
            z_part = z_sb[:, g, :, KP * f : KP * (f + 1)].rearrange("p t (q u e) -> p u t q e", u=2, e=2)
            nc.vector.tensor_scalar(
                out=mask[:], in0=z_part[:, u, :, :, :], scalar1=0.0, scalar2=None, op0=ALU.is_gt
            )
            mask_of[g, f, u] = mask

        def turn_mask(g, f, u):
            words = mask_of[g, f, u][:].rearrange("p t q e -> p (t q e)").bitcast(F32)
            turned = ps_tr.tile([P, PACK, P], F32, name="turned")
            for t in range(PACK):
                nc.tensor.transpose(turned[:, t, :], words[:, P * t : P * (t + 1)], ident[:])
            turned_mask[g, f, u] = turned

        def make_slope(g, f, u):
            pairs = turned_mask[g, f, u][:].rearrange("p t m -> p (t m)").bitcast(BF16)
            for e in range(2):
                k = 2 * u + e
                nc.scalar.activation(
                    out=slope[:, f, k, KP * g : KP * (g + 1)],
                    in_=pairs[:, e : 2 * KP : 2],
                    func=ACT.Identity,
                    bias=leak_col[:, f, k : k + 1],
                    scale=rest_col[:, f, k : k + 1],
                )

        acc2, v_of, turned_of, dz_of = {}, {}, {}, {}

        def stage2_passes(j, f):
            acc = ps_acc.tile([P, KP], F32, name="acc")
            for gk in range(MG):
                nc.tensor.matmul_mx(
                    out=acc[:],
                    lhsT=c[:, gk, 2 * P * j : 2 * P * (j + 1)].bitcast(FP4X4),
                    lhsT_scale=c_s[:, gk, P * j : P * (j + 1)],
                    rhs=d1q[:, gk, KP * f : KP * (f + 1)].bitcast(FP8X4),
                    rhs_scale=d1q_s[:, gk, KP * f : KP * (f + 1)],
                    start=(gk == 0),
                    stop=(gk == MG - 1),
                )
            acc2[j, f] = acc

        def make_v(j, f):
            g, t = divmod(j, PACK)
            v = stage.tile([P, KP], F32, name="v", bufs=4, align_bytes=64)
            nc.vector.scalar_tensor_tensor(
                out=v[:], in0=acc2[j, f][:], scalar=r_col[:, g, t : t + 1],
                in1=d1[:, g, t, KP * f : KP * (f + 1)], op0=ALU.mult, op1=ALU.add,
            )
            v_of[j, f] = v

        def turn_v(j, f):
            turned = ps_tr.tile([P, PACK, P], F32, name="turned")
            for k in range(PACK):
                nc.tensor.transpose(turned[:, k, :], v_of[j, f][:, P * k : P * (k + 1)], ident[:])
            turned_of[j, f] = turned

        def make_dz(j, f):
            if j % PAIR == 0:
                dz_of[j // PAIR, f] = stage.tile([P, PAIR, P, PACK], BF16, name="dz", bufs=2, align_bytes=64)
            nc.vector.tensor_tensor(
                out=dz_of[j // PAIR, f][:, j % PAIR, :, :],
                in0=turned_of[j, f][:].rearrange("p k m -> p m k"),
                in1=slope[:, f, :, P * j : P * (j + 1)].rearrange("p k m -> p m k"),
                op=ALU.mult,
            )

        def quantize_dz(jp, f, a, b):
            cols = slice(P * (PAIR * jp + a), P * (PAIR * jp + b))
            nc.vector.quantize_mx(
                out=dzq[:, f, cols].bitcast(FP8X4),
                scales=dzq_s[:, f, cols],
                in_=dz_of[jp, f][:, a:b, :, :].rearrange("p i m k -> p (i m k)"),
            )

        acc3 = {}

        def stage3_passes(j):
            acc = ps_acc.tile([P, F], F32, name="acc")
            for f in range(HG):
                nc.tensor.matmul_mx(
                    out=acc[:],
                    lhsT=dzq[:, f, P * j : P * (j + 1)].bitcast(FP8X4),
                    lhsT_scale=dzq_s[:, f, P * j : P * (j + 1)],
                    rhs=at[:, f, :].bitcast(FP4X4),
                    rhs_scale=at_s[:, f, :],
                    start=(f == 0),
                    stop=(f == HG - 1),
                )
            acc3[j] = acc

        def store(j):
            g, t = divmod(j, PACK)
            res = stage.tile([P, F], F32, name="res", bufs=4, align_bytes=64)
            nc.scalar.copy(out=res[:], in_=acc3[j][:])
            nc.sync.dma_start(out=out_v[g][:, t, :], in_=res[:])

        blocks = [(0, 0), (0, 1), (1, 0), (1, 1), (0, 2), (1, 2)]
        plan = []

        def at_tick(tick, step, *args):
            plan.append((tick, step, args))

        dy_tick = {(0, 0): 2, (0, 1): 14, (0, 2): 20, (1, 0): 41, (1, 1): 49, (1, 2): 55}
        halves = [(g, f, half) for g in range(MG) for f in range(HG) for half in range(2)]
        for g, f, half in halves:
            at_tick(dy_tick[g, f] + 1 * half, turn_dy, g, f, half)
        for g, f, half in halves:
            at_tick(dy_tick[g, f] + 1 * half, group_dy, g, f, half)
        for g, f, half in halves:
            at_tick(dy_tick[g, f] + 1 * half + (6, 11)[g], quantize_dy, g, f, half)
        for f in range(HG):
            for t in range(PACK):
                at_tick((10, 26, 33)[f], stage1_pass, 0, 0, t, f)
        block_tick = (45, 58, 109, 145, 187, 169)
        add_tick = {}
        for b in range(1, len(blocks)):
            for t in range(PACK):
                at_tick(block_tick[b] + 3 * t, stage1_passes, *blocks[b], t)
        for b in range(len(blocks)):
            for t in range(PACK):
                add_tick[b] = block_tick[b] + (t if b == 0 else 3 * t + 20)
                at_tick(add_tick[b], add_dy, *blocks[b], t)
        for b in range(len(blocks)):
            at_tick(add_tick[b] + 22, round_d1, *blocks[b])
        for b in range(len(blocks)):
            at_tick(add_tick[b] + 51, quantize_d1, *blocks[b])
        for g in range(MG):
            for gk in range(MG):
                at_tick((61, 137)[g] + 2 * gk, order_c_words, gk, g)
        for gk in range(MG):
            at_tick(157 + 2 * gk, order_c_scales, gk)
        units = [(j, f) for f in range(HG) for j in range(M // P)]
        chunk_tick = (206, 240, 268)
        mask_tick = {(0, 0): 129, (1, 0): 207, (0, 1): 115, (1, 1): 229, (0, 2): 241, (1, 2): 255}
        parts = [(g, f, u) for g in range(MG) for f in range(HG) for u in range(2)]
        for j, f in units:
            at_tick(chunk_tick[f] + 4 * j + (-1), scale_d1, j, f)
        for lag, step in ((0, make_mask), (14, turn_mask), (17, make_slope)):
            for g, f, u in parts:
                at_tick(mask_tick[g, f] + 7 * u + lag, step, g, f, u)
        for lag, step in ((0, stage2_passes), (11, make_v), (12, turn_v), (19, make_dz)):
            for j, f in units:
                at_tick(chunk_tick[f] + 4 * j + lag, step, j, f)
        for f in range(HG):
            for jp in range(M // P // PAIR):
                tick = chunk_tick[f] + 4 * (PAIR * jp + 1) + 24
                if f < HG - 1 or jp < M // P // PAIR - 1:
                    at_tick(tick, quantize_dz, jp, f, 0, PAIR)
        for i in range(PAIR):
            at_tick(chunk_tick[2] + 4 * (M // P - PAIR + i) + 24, quantize_dz, M // P // PAIR - 1, 2, i, i + 1)
        for step in (stage3_passes, store):
            for j in range(M // P):
                last = j if j >= M // P - PAIR else PAIR * (j // PAIR) + 1
                at_tick(chunk_tick[2] + 4 * last + 24, step, j)
        for tick, step, args in sorted(plan, key=lambda entry: entry[0]):
            step(*args)
